import numpy as np
import ml_dtypes


def mxq(x, axis, fmt="e4m3"):
    dtype, down = {"e4m3": (ml_dtypes.float8_e4m3fn, 7), "e5m2": (ml_dtypes.float8_e5m2, 14)}[fmt]
    v = np.moveaxis(np.asarray(x, np.float32).astype(ml_dtypes.bfloat16).astype(np.float64), axis, -1)
    blocks = v.reshape(v.shape[:-1] + (-1, 32))
    amax = np.abs(blocks).max(-1, keepdims=True)
    byte = np.maximum(np.where(amax > 0, np.frexp(amax)[1] - 1 + 127, 0) - down, 1)
    scale = np.exp2(byte - 127.0)
    codes = (blocks / scale).astype(np.float32).astype(dtype).astype(np.float64)
    return np.moveaxis((codes * scale).reshape(v.shape), -1, axis)


WIDE = False


def mx_kscale(k):
    if not WIDE:
        return np.ones(k)
    levels = np.array([10, -10, 5, -5, 0])
    if k % 512:
        return np.exp2(np.random.permutation(np.resize(levels, k // 32))).repeat(32)
    a = np.empty((k // 512, 16))
    for p in range(k // 512):
        a[p, :8] = np.random.permutation(np.resize(levels, 8))
        for g in range(8):
            far = levels[np.abs(levels - a[p, g]) >= 10]
            a[p, g + 8] = far[np.random.randint(len(far))]
    return np.exp2(a.ravel()).repeat(32)


def f64(x):
    return np.asarray(x).astype(np.float64)


def striped(idx):
    return np.tile(np.asarray(idx).reshape(-1, 16).T, (8, 1)).astype(np.uint16)


def unstriped(offs):
    return offs[:16].T.reshape(-1).astype(np.int64)


E2M1 = np.array([0.0, 0.5, 1.0, 1.5, 2.0, 3.0, 4.0, 6.0, -0.0, -0.5, -1.0, -1.5, -2.0, -3.0, -4.0, -6.0])


def pack_weight(w, fmt):
    k, n = w.shape
    w = f64(np.asarray(w, np.float32).astype(ml_dtypes.bfloat16)).reshape(k // 32, 32, n)
    amax = np.abs(w).max(1)
    if fmt == "e4m3":
        byte = np.frexp(amax)[1] - 1 + 127 - 7
    else:
        mant, ex = np.frexp(amax / 6.0)
        byte = np.where(mant > 0.5, ex, ex - 1) + 127
    byte = np.clip(np.where(amax > 0, byte, 1), 1, 254)
    scaled = (w * np.exp2(127.0 - byte)[:, None, :]).reshape(k, n).astype(np.float32)
    by_word = np.ascontiguousarray(scaled.reshape(k // 512, 128, 4, n).transpose(0, 1, 3, 2))
    if fmt == "e4m3":
        words = by_word.astype(ml_dtypes.float8_e4m3fn).view(np.uint8)
    else:
        c = by_word.astype(ml_dtypes.float4_e2m1fn).view(np.uint8) & 0xF
        words = (c[..., 0::2] | (c[..., 1::2] << 4)).reshape(k // 512, 128, 2 * n)
    return np.ascontiguousarray(words), np.ascontiguousarray(byte.astype(np.uint8).reshape(k // 512, 16, n))


def unpack_weight(words, scales, fmt):
    g, _, n = scales.shape
    words = np.ascontiguousarray(words).reshape(g, 128, n, -1)
    if fmt == "e4m3":
        vals = words.view(ml_dtypes.float8_e4m3fn).astype(np.float64)
    else:
        nib = np.empty((g, 128, n, 4), np.uint8)
        nib[..., 0::2] = words & 0xF
        nib[..., 1::2] = words >> 4
        vals = E2M1[nib]
    vals = vals * np.repeat(np.exp2(scales.astype(np.float64) - 127.0), 8, axis=1)[..., None]
    return vals.transpose(0, 1, 3, 2).reshape(g * 512, n)


D, E, T, I, Q = 512, 512, 2048, 512, 128


def setup_inputs():
    n = np.random.standard_normal
    idx2 = np.random.permutation(I)[:I]
    idx = np.random.permutation(T)[:I]
    fd = mx_kscale(D)
    fi = mx_kscale(I)
    ti = np.ones(T)
    ti[idx] = fi
    keysp = pack_weight(n((D, T)) / fd[:, None], "e2m1")
    return {
        "query": (n((D, Q)) * 0.7 / np.sqrt(D) * fd[:, None]).astype(np.float32),
        "keys_words": keysp[0],
        "keys_scales": keysp[1],
        "dquery": (n((D, Q)) * 0.6 / np.sqrt(D) * fd[:, None]).astype(np.float32),
        "os": (np.random.uniform(4.0, 16.0, (1, I)) * fi).astype(np.float32),
        "vals": (n((E, T)) / ti).astype(np.float32),
        "offs2": striped(idx2),
        "offs": striped(idx),
    }


def reference(query, keys_words, keys_scales, dquery, os, vals, offs2, offs):
    idx2 = unstriped(offs2)
    idx = unstriped(offs)
    keysu = unpack_weight(keys_words, keys_scales, "e2m1")
    queryq = mxq(f64(query), 0, "e4m3")
    keysidxg = keysu[:, idx]
    a = queryq.T @ keysidxg
    dqueryq = mxq(f64(dquery), 0, "e4m3")
    ta = dqueryq.T @ keysidxg
    pa = np.exp(a)
    pb = np.sqrt(pa)
    p = pa * pb[:, idx2]
    z = np.sum(p, axis=1, keepdims=True)
    tpa = ta * pa
    tpb = tpa * 0.5 / pb
    tp = tpa * pb[:, idx2] + tpb[:, idx2] * pa
    tz = np.sum(tp, axis=1, keepdims=True)
    tw = (tp - tz * p / z) / z
    wo1 = tw * f64(os)
    wt1 = wo1.T
    vt1 = f64(vals)[:, idx].T
    wt1q = mxq(wt1, 0, "e4m3")
    vt1q = mxq(vt1, 0, "e4m3")
    o = wt1q.T @ vt1q
    return o

@@ -1,0 +1,187 @@
+from contextlib import ExitStack
+
+import concourse.mybir as mybir
+from concourse.masks import make_identity
+
+F32 = mybir.dt.float32
+BF16 = mybir.dt.bfloat16
+I32 = mybir.dt.int32
+U32 = mybir.dt.uint32
+U16 = mybir.dt.uint16
+U8 = mybir.dt.uint8
+FP8X4 = mybir.dt.float8_e4m3fn_x4
+FP4X4 = mybir.dt.float4_e2m1fn_x4
+ALU = mybir.AluOpType
+ACT = mybir.ActivationFunctionType
+
+P = 128
+PACK = 4
+D, E, T, SLOTS, Q = 512, 512, 2048, 512, 128
+FLOPS = 2 * (2 * D * Q * SLOTS) + 2 * SLOTS * Q * E
+LIST_COLS = SLOTS // 16
+HALF = SLOTS // 2
+LARGEST = 3.0e38
+
+
+def tile_attend_ttlinkedproduct_kernel(tc, query, keys_words, keys_scales, dquery, slot_factor, vals, offs2, offs, out):
+    nc = tc.nc
+    with ExitStack() as ctx:
+        sb = ctx.enter_context(tc.tile_pool(name="sb", bufs=1))
+        ps = ctx.enter_context(tc.psum_pool(name="ps", bufs=1))
+
+        offs_t = sb.tile([P, LIST_COLS], U16, name="offs_t")
+        offs2_t = sb.tile([P, LIST_COLS], U16, name="offs2_t")
+        kw = sb.tile([P, T], U16, name="kw")
+        ks = sb.tile([P, T], U8, name="ks")
+        q_raw = [sb.tile([P, PACK, Q], F32, name="q_raw%d" % n) for n in range(2)]
+        os4 = sb.tile([P, PACK], F32, name="os4")
+        v_raw = [sb.tile([P, T], F32, name="v_raw%d" % j, tag="v_raw%d" % j, align_bytes=64) for j in range(4)]
+        ident = sb.tile([P, P], F32, name="ident")
+
+
+        nc.gpsimd.memset(ks[:].bitcast(I32), 0)
+        make_identity(nc, ident[:])
+
+        nc.sync.dma_start(offs_t[:], offs)
+        nc.sync.dma_start(kw[:].bitcast(I32), keys_words[0].bitcast(I32))
+        for g in range(4):
+            nc.sync.dma_start(ks[32 * g : 32 * g + 4, :].bitcast(I32), keys_scales[0, 4 * g : 4 * g + 4, :].bitcast(I32))
+        for n, src in enumerate((query, dquery)):
+            nc.sync.dma_start(q_raw[n][:], src.rearrange("(p j) w -> p j w", j=PACK))
+        nc.sync.dma_start(v_raw[0][:], vals[0:P, :])
+        nc.sync.dma_start(offs2_t[:], offs2)
+        nc.sync.dma_start(os4[:], slot_factor.rearrange("o (p t) -> (o p) t", t=PACK))
+        for j in range(1, 4):
+            nc.sync.dma_start(v_raw[j][:], vals[j * P : (j + 1) * P, :])
+
+        h = LIST_COLS // 2
+        halves = [(slice(s * HALF, (s + 1) * HALF), slice(s * h, (s + 1) * h)) for s in range(2)]
+
+        def wide(name):
+            return sb.tile([P, SLOTS], F32, name=name)
+
+        def column(name):
+            return sb.tile([P, 1], F32, name=name)
+
+        def quantise(grouped, codes, plane):
+            nc.vector.quantize_mx(out=codes.bitcast(FP8X4), scales=plane, in_=grouped[:].rearrange("p w j -> p (w j)"))
+
+        def product(acc, codes, plane, moving, moving_plane):
+            nc.tensor.matmul_mx(out=acc, lhsT=codes[:].bitcast(FP8X4), lhsT_scale=plane[:], rhs=moving, rhs_scale=moving_plane,
+                                start=True, stop=True)
+
+        ksg = sb.tile([P, SLOTS], U8, name="ksg", align_bytes=64)
+        kwg = sb.tile([P, SLOTS], U16, name="kwg", align_bytes=64)
+        q_grouped = [sb.tile([P, Q, PACK], BF16, name="q_grouped%d" % n, align_bytes=64) for n in range(2)]
+        q_codes = [sb.tile([P, Q], U32, name="q_codes%d" % n, align_bytes=64) for n in range(2)]
+        q_plane = [sb.tile([P, Q], U8, name="q_plane%d" % n, align_bytes=64) for n in range(2)]
+        a = [ps.tile([P, HALF], F32, name="a%d" % s, tag="shared%d" % s) for s in range(2)]
+        ta = ps.tile([P, SLOTS], F32, name="ta")
+
+        nc.vector.tensor_copy(kwg[:], kw[:].indirect(offs_t[:]))
+        for s, (cols, entries) in enumerate(halves):
+            nc.scalar.copy(q_grouped[s][:], q_raw[s][:].rearrange("p j w -> p w j"))
+            quantise(q_grouped[s], q_codes[s][:], q_plane[s][:])
+            nc.vector.tensor_copy(ksg[:, cols], ks[:].indirect(offs_t[:, entries]))
+            product(a[s][:], q_codes[0], q_plane[0], kwg[:, cols].bitcast(FP4X4), ksg[:, cols])
+        product(ta[:], q_codes[1], q_plane[1], kwg[:].bitcast(FP4X4), ksg[:])
+
+        os_rows = ps.tile([P, PACK, P], F32, name="os_rows")
+        for t in range(PACK):
+            nc.tensor.transpose(os_rows[:, t, :], os4[:, t : t + 1].to_broadcast([P, P]), ident[:])
+
+        v_codes = sb.tile([P, E], U32, name="v_codes", align_bytes=64)
+        v_plane = sb.tile([P, E], U8, name="v_plane", align_bytes=64)
+
+        def weave(copy, turned, name, tag):
+            grouped = sb.tile([P, P, PACK], BF16, name=name + "_grouped", tag=tag, align_bytes=64)
+            copy(grouped[:].bitcast(F32), turned[:].rearrange("p u r -> p r u"))
+            return grouped
+
+        picked = {j: sb.tile([P, SLOTS], BF16, name="v_picked%d" % j) for j in range(1, 4)}
+
+        def pick_scalar(j):
+            nc.scalar.activation(picked[j][:], v_raw[j][:].indirect(offs_t[:]), ACT.Copy)
+
+        def turn(j):
+            words = picked[j][:].bitcast(F32)
+            turned = ps.tile([P, 2, P], F32, name="v%d_ps" % j, tag="v_bank%d" % (j % 2))
+            for u in range(2):
+                nc.tensor.transpose(turned[:, u, :], words[:, u : HALF : 2], ident[:])
+            return turned
+
+        def quantise_values(j, grouped):
+            cols = slice(j * P, (j + 1) * P)
+            quantise(grouped, v_codes[:, cols], v_plane[:, cols])
+
+        neg_half_a = wide("neg_half_a")
+        shift = LARGEST
+        for s, (cols, entries) in enumerate(halves):
+            least = sb.tile([P, 1], F32, name="least%d" % s, tag="least%d" % s)
+            nc.vector.tensor_scalar(neg_half_a[:, cols], a[s][:], -0.5, shift, ALU.mult, ALU.min, accum_out=least[:])
+            shift = least[:]
+        picked.setdefault(0, sb.tile([P, SLOTS], BF16, name="v_picked0", tag="least0"))
+        nc.vector.tensor_copy(picked[0][:], v_raw[0][:].indirect(offs_t[:]))
+        pb = wide("pb")
+        nc.scalar.activation(pb[:], neg_half_a[:], ACT.Exp, bias=shift, scale=-1.0)
+
+        tpb = sb.tile([P, SLOTS], F32, name="tpb", tag="v_raw0", align_bytes=64)
+        nc.vector.scalar_tensor_tensor(tpb[:], ta[:], 0.5, pb[:], ALU.mult, ALU.mult)
+        pa = wide("pa")
+        nc.scalar.activation(pa[:], pb[:], ACT.Square)
+        v0_grouped = weave(nc.vector.tensor_copy, turn(0), "v0", "v0_grouped")
+        pb_linked = wide("pb_linked")
+        linked = wide("linked")
+        for cols, entries in halves:
+            nc.scalar.activation(pb_linked[:, cols], pb[:].indirect(offs2_t[:, entries]), ACT.Copy)
+        for j in range(1, 4):
+            pick_scalar(j)
+
+
+        def link(s):
+            cols, entries = halves[s]
+            nc.vector.tensor_tensor(linked[:, cols], tpb[:].indirect(offs2_t[:, entries]), pa[:, cols], ALU.mult)
+
+        p, z = wide("p"), column("z")
+        link(0)
+        link(1)
+        nc.vector.scalar_tensor_tensor(p[:], pb_linked[:], 1.0, pa[:], ALU.mult, ALU.mult, accum_out=z[:])
+        quantise_values(0, v0_grouped)
+        own = wide("own")
+        nc.vector.tensor_tensor(own[:], ta[:], p[:], ALU.mult)
+        inv_z = column("inv_z")
+        nc.vector.reciprocal(inv_z[:], z[:])
+        tp, tz = wide("tp"), column("tz")
+        nc.vector.scalar_tensor_tensor(tp[:], own[:], 1.0, linked[:], ALU.mult, ALU.add, accum_out=tz[:])
+
+        neg_ratio = column("neg_ratio")
+        nc.vector.tensor_scalar(neg_ratio[:], tz[:], inv_z[:], -1.0, ALU.mult, ALU.mult)
+        v1_grouped = weave(nc.vector.tensor_copy, turn(1), "v1", "v1_grouped")
+        centred = wide("centred")
+        nc.vector.scalar_tensor_tensor(centred[:], p[:], neg_ratio[:], tp[:], ALU.mult, ALU.add)
+
+        quantise_values(1, v1_grouped)
+        w = sb.tile([P, 2, P, 2], BF16, name="w")
+        w_turned = ps.tile([P, 2, P], F32, name="w_turned")
+        by_place = centred[:].rearrange("q (s t) -> q s t", t=PACK)
+        for u in range(2):
+            nc.vector.scalar_tensor_tensor(w[:, u, :, :], by_place[:, :, 2 * u : 2 * u + 2], inv_z[:],
+                                           os_rows[:, 2 * u : 2 * u + 2, :].rearrange("q t s -> q s t"), ALU.mult, ALU.mult)
+            nc.tensor.transpose(w_turned[:, u, :], w[:, u, :, :].rearrange("q s e -> q (s e)").bitcast(F32), ident[:])
+        quantise_values(2, weave(nc.vector.tensor_copy, turn(2), "v2", "v2_grouped"))
+        w_codes = sb.tile([P, Q], U32, name="w_codes", align_bytes=64)
+        w_plane = sb.tile([P, Q], U8, name="w_plane", align_bytes=64)
+        w_grouped = weave(nc.scalar.copy, w_turned, "w", "v_raw3")
+
+        quantise(w_grouped, w_codes[:], w_plane[:])
+        quantise_values(3, weave(nc.scalar.copy, turn(3), "v3", "v3_grouped"))
+
+        result = sb.tile([P, E], F32, name="result")
+        early = ps.tile([P, 3 * P], F32, name="early", tag="shared0")
+        late = ps.tile([P, P], F32, name="late", tag="shared1")
+        for acc, cols in ((early[:, : 2 * P], slice(0, 2 * P)), (early[:, 2 * P :], slice(2 * P, 3 * P)), (late[:], slice(3 * P, E))):
+            product(acc, w_codes, w_plane, v_codes[:, cols].bitcast(FP8X4), v_plane[:, cols])
+        nc.scalar.copy(result[:, : 3 * P], early[:])
+        nc.scalar.dma_start(out[:, : 3 * P], result[:, : 3 * P])
+        nc.vector.tensor_copy(result[:, 3 * P :], late[:])
+        nc.sync.dma_start(out[:, 3 * P :], result[:, 3 * P :])

@@ -20,13 +20,14 @@ D, E, T, SLOTS, Q = 512, 512, 2048, 512, 128
 FLOPS = 2 * (2 * D * Q * SLOTS) + 2 * SLOTS * Q * E
 LIST_COLS = SLOTS // 16
 HALF = SLOTS // 2
-LARGEST = 3.0e38
+ROW_BYTES = 4 * SLOTS
 
 
 def tile_attend_ttlinkedproduct_kernel(tc, query, keys_words, keys_scales, dquery, slot_factor, vals, offs2, offs, out):
     nc = tc.nc
     with ExitStack() as ctx:
         sb = ctx.enter_context(tc.tile_pool(name="sb", bufs=1))
+        reuse = ctx.enter_context(tc.tile_pool(name="reuse", bufs=1))
         ps = ctx.enter_context(tc.psum_pool(name="ps", bufs=1))
 
         offs_t = sb.tile([P, LIST_COLS], U16, name="offs_t")
@@ -35,7 +36,7 @@ def tile_attend_ttlinkedproduct_kernel(tc, query, keys_words, keys_scales, dquer
         ks = sb.tile([P, T], U8, name="ks")
         q_raw = [sb.tile([P, PACK, Q], F32, name="q_raw%d" % n) for n in range(2)]
         os4 = sb.tile([P, PACK], F32, name="os4")
-        v_raw = [sb.tile([P, T], F32, name="v_raw%d" % j, tag="v_raw%d" % j, align_bytes=64) for j in range(4)]
+        v_raw = [reuse.tile([P, T], F32, name="v_raw0", offset=0)] + [sb.tile([P, T], F32, name="v_raw%d" % j, tag="v_raw%d" % j, align_bytes=64) for j in range(1, 4)]
         ident = sb.tile([P, P], F32, name="ident")
 
 
@@ -43,13 +44,13 @@ def tile_attend_ttlinkedproduct_kernel(tc, query, keys_words, keys_scales, dquer
         make_identity(nc, ident[:])
 
         nc.sync.dma_start(offs_t[:], offs)
-        nc.sync.dma_start(kw[:].bitcast(I32), keys_words[0].bitcast(I32))
-        for g in range(4):
-            nc.sync.dma_start(ks[32 * g : 32 * g + 4, :].bitcast(I32), keys_scales[0, 4 * g : 4 * g + 4, :].bitcast(I32))
-        for n, src in enumerate((query, dquery)):
-            nc.sync.dma_start(q_raw[n][:], src.rearrange("(p j) w -> p j w", j=PACK))
-        nc.sync.dma_start(v_raw[0][:], vals[0:P, :])
         nc.sync.dma_start(offs2_t[:], offs2)
+        nc.sync.dma_start(kw[:].bitcast(I32), keys_words[0].bitcast(I32))
+        nc.sync.dma_start(q_raw[0][:], query.rearrange("(p j) w -> p j w", j=PACK))
+        for r in range(4):
+            nc.sync.dma_start(ks[r:P:32, :].bitcast(I32), keys_scales[0, r:16:4, :].bitcast(I32))
+        nc.sync.dma_start(q_raw[1][:], dquery.rearrange("(p j) w -> p j w", j=PACK))
+        nc.sync.dma_start(v_raw[0][:], vals[0:P, :])
         nc.sync.dma_start(os4[:], slot_factor.rearrange("o (p t) -> (o p) t", t=PACK))
         for j in range(1, 4):
             nc.sync.dma_start(v_raw[j][:], vals[j * P : (j + 1) * P, :])
@@ -64,124 +65,107 @@ def tile_attend_ttlinkedproduct_kernel(tc, query, keys_words, keys_scales, dquer
             return sb.tile([P, 1], F32, name=name)
 
         def quantise(grouped, codes, plane):
-            nc.vector.quantize_mx(out=codes.bitcast(FP8X4), scales=plane, in_=grouped[:].rearrange("p w j -> p (w j)"))
+            nc.vector.quantize_mx(out=codes.bitcast(FP8X4), scales=plane, in_=grouped.rearrange("p w j -> p (w j)"))
 
         def product(acc, codes, plane, moving, moving_plane):
-            nc.tensor.matmul_mx(out=acc, lhsT=codes[:].bitcast(FP8X4), lhsT_scale=plane[:], rhs=moving, rhs_scale=moving_plane,
+            nc.tensor.matmul_mx(out=acc, lhsT=codes.bitcast(FP8X4), lhsT_scale=plane, rhs=moving, rhs_scale=moving_plane,
                                 start=True, stop=True)
 
-        ksg = sb.tile([P, SLOTS], U8, name="ksg", align_bytes=64)
         kwg = sb.tile([P, SLOTS], U16, name="kwg", align_bytes=64)
+        ksg = [sb.tile([P, HALF], U8, name="ksg%d" % s, align_bytes=64) for s in range(2)]
         q_grouped = [sb.tile([P, Q, PACK], BF16, name="q_grouped%d" % n, align_bytes=64) for n in range(2)]
         q_codes = [sb.tile([P, Q], U32, name="q_codes%d" % n, align_bytes=64) for n in range(2)]
         q_plane = [sb.tile([P, Q], U8, name="q_plane%d" % n, align_bytes=64) for n in range(2)]
-        a = [ps.tile([P, HALF], F32, name="a%d" % s, tag="shared%d" % s) for s in range(2)]
-        ta = ps.tile([P, SLOTS], F32, name="ta")
+        a = ps.tile([P, SLOTS], F32, name="a", tag="bank_a")
+        ta = ps.tile([P, SLOTS], F32, name="ta", tag="bank_ta")
 
         nc.vector.tensor_copy(kwg[:], kw[:].indirect(offs_t[:]))
+        for n in range(2):
+            nc.scalar.copy(q_grouped[n][:], q_raw[n][:].rearrange("p j w -> p w j"))
+        quantise(q_grouped[0][:], q_codes[0][:], q_plane[0][:])
         for s, (cols, entries) in enumerate(halves):
-            nc.scalar.copy(q_grouped[s][:], q_raw[s][:].rearrange("p j w -> p w j"))
-            quantise(q_grouped[s], q_codes[s][:], q_plane[s][:])
-            nc.vector.tensor_copy(ksg[:, cols], ks[:].indirect(offs_t[:, entries]))
-            product(a[s][:], q_codes[0], q_plane[0], kwg[:, cols].bitcast(FP4X4), ksg[:, cols])
-        product(ta[:], q_codes[1], q_plane[1], kwg[:].bitcast(FP4X4), ksg[:])
+            nc.vector.tensor_copy(ksg[s][:], ks[:].indirect(offs_t[:, entries]))
+            product(a[:, cols], q_codes[0][:], q_plane[0][:], kwg[:, cols].bitcast(FP4X4), ksg[s][:])
+        quantise(q_grouped[1][:], q_codes[1][:], q_plane[1][:])
+        for s, (cols, entries) in enumerate(halves):
+            product(ta[:, cols], q_codes[1][:], q_plane[1][:], kwg[:, cols].bitcast(FP4X4), ksg[s][:])
 
         os_rows = ps.tile([P, PACK, P], F32, name="os_rows")
         for t in range(PACK):
             nc.tensor.transpose(os_rows[:, t, :], os4[:, t : t + 1].to_broadcast([P, P]), ident[:])
 
-        v_codes = sb.tile([P, E], U32, name="v_codes", align_bytes=64)
-        v_plane = sb.tile([P, E], U8, name="v_plane", align_bytes=64)
+        v_plane = [sb.tile([P, HALF], U8, name="v_plane%d" % s, align_bytes=64) for s in range(2)]
+        picked = [sb.tile([P, SLOTS], BF16, name="v_picked%d" % j) for j in range(4)]
 
-        def weave(copy, turned, name, tag):
-            grouped = sb.tile([P, P, PACK], BF16, name=name + "_grouped", tag=tag, align_bytes=64)
-            copy(grouped[:].bitcast(F32), turned[:].rearrange("p u r -> p r u"))
-            return grouped
+        def weave(copy, turned, grouped):
+            copy(grouped.bitcast(F32), turned[:].rearrange("p u r -> p r u"))
 
-        picked = {j: sb.tile([P, SLOTS], BF16, name="v_picked%d" % j) for j in range(1, 4)}
-
-        def pick_scalar(j):
-            nc.scalar.activation(picked[j][:], v_raw[j][:].indirect(offs_t[:]), ACT.Copy)
-
-        def turn(j):
+        def turn(j, bank):
             words = picked[j][:].bitcast(F32)
-            turned = ps.tile([P, 2, P], F32, name="v%d_ps" % j, tag="v_bank%d" % (j % 2))
+            turned = ps.tile([P, 2, P], F32, name="v%d_turned" % j, tag=bank)
             for u in range(2):
                 nc.tensor.transpose(turned[:, u, :], words[:, u : HALF : 2], ident[:])
             return turned
 
-        def quantise_values(j, grouped):
-            cols = slice(j * P, (j + 1) * P)
-            quantise(grouped, v_codes[:, cols], v_plane[:, cols])
-
-        neg_half_a = wide("neg_half_a")
-        shift = LARGEST
-        for s, (cols, entries) in enumerate(halves):
-            least = sb.tile([P, 1], F32, name="least%d" % s, tag="least%d" % s)
-            nc.vector.tensor_scalar(neg_half_a[:, cols], a[s][:], -0.5, shift, ALU.mult, ALU.min, accum_out=least[:])
-            shift = least[:]
-        picked.setdefault(0, sb.tile([P, SLOTS], BF16, name="v_picked0", tag="least0"))
         nc.vector.tensor_copy(picked[0][:], v_raw[0][:].indirect(offs_t[:]))
-        pb = wide("pb")
-        nc.scalar.activation(pb[:], neg_half_a[:], ACT.Exp, bias=shift, scale=-1.0)
+        pb, pb_sum = wide("pb"), column("pb_sum")
+        nc.scalar.activation(pb[:], a[:], ACT.Exp, scale=0.5, accum_out=pb_sum[:])
 
-        tpb = sb.tile([P, SLOTS], F32, name="tpb", tag="v_raw0", align_bytes=64)
+        norm = reuse.tile([P, 1], F32, name="norm", offset=ROW_BYTES)
+        nc.vector.reciprocal(norm[:], pb_sum[:])
+        tpb = reuse.tile([P, SLOTS], F32, name="tpb", offset=0)
         nc.vector.scalar_tensor_tensor(tpb[:], ta[:], 0.5, pb[:], ALU.mult, ALU.mult)
         pa = wide("pa")
-        nc.scalar.activation(pa[:], pb[:], ACT.Square)
-        v0_grouped = weave(nc.vector.tensor_copy, turn(0), "v0", "v0_grouped")
-        pb_linked = wide("pb_linked")
-        linked = wide("linked")
+        nc.scalar.activation(pa[:], pb[:], ACT.Square, scale=norm[:])
+        pb_linked = reuse.tile([P, SLOTS], F32, name="pb_linked", offset=ROW_BYTES)
         for cols, entries in halves:
             nc.scalar.activation(pb_linked[:, cols], pb[:].indirect(offs2_t[:, entries]), ACT.Copy)
+        early_grouped = sb.tile([P, 2 * P, PACK], BF16, name="early_grouped", align_bytes=64)
+        weave(nc.scalar.copy, turn(0, "bank_v"), early_grouped[:, :P, :])
         for j in range(1, 4):
-            pick_scalar(j)
+            nc.scalar.activation(picked[j][:], v_raw[j][:].indirect(offs_t[:]), ACT.Copy)
 
-
-        def link(s):
-            cols, entries = halves[s]
+        linked = wide("linked")
+        for cols, entries in halves:
             nc.vector.tensor_tensor(linked[:, cols], tpb[:].indirect(offs2_t[:, entries]), pa[:, cols], ALU.mult)
-
         p, z = wide("p"), column("z")
-        link(0)
-        link(1)
         nc.vector.scalar_tensor_tensor(p[:], pb_linked[:], 1.0, pa[:], ALU.mult, ALU.mult, accum_out=z[:])
-        quantise_values(0, v0_grouped)
-        own = wide("own")
-        nc.vector.tensor_tensor(own[:], ta[:], p[:], ALU.mult)
         inv_z = column("inv_z")
         nc.vector.reciprocal(inv_z[:], z[:])
+        own = wide("own")
+        nc.vector.tensor_tensor(own[:], ta[:], p[:], ALU.mult)
         tp, tz = wide("tp"), column("tz")
         nc.vector.scalar_tensor_tensor(tp[:], own[:], 1.0, linked[:], ALU.mult, ALU.add, accum_out=tz[:])
-
+        weave(nc.vector.tensor_copy, turn(1, "bank_ta"), early_grouped[:, P:, :])
         neg_ratio = column("neg_ratio")
         nc.vector.tensor_scalar(neg_ratio[:], tz[:], inv_z[:], -1.0, ALU.mult, ALU.mult)
-        v1_grouped = weave(nc.vector.tensor_copy, turn(1), "v1", "v1_grouped")
-        centred = wide("centred")
+        centred = sb.tile([P, SLOTS], F32, name="centred", tag="centred", align_bytes=64)
         nc.vector.scalar_tensor_tensor(centred[:], p[:], neg_ratio[:], tp[:], ALU.mult, ALU.add)
 
-        quantise_values(1, v1_grouped)
         w = sb.tile([P, 2, P, 2], BF16, name="w")
         w_turned = ps.tile([P, 2, P], F32, name="w_turned")
         by_place = centred[:].rearrange("q (s t) -> q s t", t=PACK)
+        v2_turned = turn(2, "bank_v")
         for u in range(2):
             nc.vector.scalar_tensor_tensor(w[:, u, :, :], by_place[:, :, 2 * u : 2 * u + 2], inv_z[:],
                                            os_rows[:, 2 * u : 2 * u + 2, :].rearrange("q t s -> q s t"), ALU.mult, ALU.mult)
             nc.tensor.transpose(w_turned[:, u, :], w[:, u, :, :].rearrange("q s e -> q (s e)").bitcast(F32), ident[:])
-        quantise_values(2, weave(nc.vector.tensor_copy, turn(2), "v2", "v2_grouped"))
+        v_codes = [sb.tile([P, HALF], U32, name="v_codes%d" % s, tag=("centred", "late_codes")[s], align_bytes=64) for s in range(2)]
+        quantise(early_grouped[:], v_codes[0][:], v_plane[0][:])
+        late_grouped = sb.tile([P, 2 * P, PACK], BF16, name="late_grouped", tag="v_raw3", align_bytes=64)
+        weave(nc.scalar.copy, v2_turned, late_grouped[:, :P, :])
+        w_grouped = sb.tile([P, P, PACK], BF16, name="w_grouped", align_bytes=64)
+        weave(nc.vector.tensor_copy, w_turned, w_grouped[:])
         w_codes = sb.tile([P, Q], U32, name="w_codes", align_bytes=64)
         w_plane = sb.tile([P, Q], U8, name="w_plane", align_bytes=64)
-        w_grouped = weave(nc.scalar.copy, w_turned, "w", "v_raw3")
-
-        quantise(w_grouped, w_codes[:], w_plane[:])
-        quantise_values(3, weave(nc.scalar.copy, turn(3), "v3", "v3_grouped"))
+        quantise(w_grouped[:], w_codes[:], w_plane[:])
+        weave(nc.scalar.copy, turn(3, "bank_a"), late_grouped[:, P:, :])
+        quantise(late_grouped[:], v_codes[1][:], v_plane[1][:])
 
         result = sb.tile([P, E], F32, name="result")
-        early = ps.tile([P, 3 * P], F32, name="early", tag="shared0")
-        late = ps.tile([P, P], F32, name="late", tag="shared1")
-        for acc, cols in ((early[:, : 2 * P], slice(0, 2 * P)), (early[:, 2 * P :], slice(2 * P, 3 * P)), (late[:], slice(3 * P, E))):
-            product(acc, w_codes, w_plane, v_codes[:, cols].bitcast(FP8X4), v_plane[:, cols])
-        nc.scalar.copy(result[:, : 3 * P], early[:])
-        nc.scalar.dma_start(out[:, : 3 * P], result[:, : 3 * P])
-        nc.vector.tensor_copy(result[:, 3 * P :], late[:])
-        nc.sync.dma_start(out[:, 3 * P :], result[:, 3 * P :])
+        for s, (bank, copy, queue) in enumerate((("bank_a", nc.scalar.copy, nc.scalar), ("bank_late", nc.vector.tensor_copy, nc.sync))):
+            cols = halves[s][0]
+            acc = ps.tile([P, HALF], F32, name="acc%d" % s, tag=bank)
+            product(acc[:], w_codes[:], w_plane[:], v_codes[s][:].bitcast(FP8X4), v_plane[s][:])
+            copy(result[:, cols], acc[:])
+            queue.dma_start(out[:, cols], result[:, cols])

@@ -16,47 +16,56 @@ ACT = mybir.ActivationFunctionType
 
 P = 128
 PACK = 4
+QUADRANT = 32
 D, E, T, SLOTS, Q = 512, 512, 2048, 512, 128
 FLOPS = 2 * (2 * D * Q * SLOTS) + 2 * SLOTS * Q * E
+VALUE_TILES = E // P
+LAST = VALUE_TILES - 1
 LIST_COLS = SLOTS // 16
 HALF = SLOTS // 2
+POOL_BYTES = 4 * T
 ROW_BYTES = 4 * SLOTS
+GROUPED_BYTES = 2 * P * PACK
+SCALAR_COLS = 22
 
 
 def tile_attend_ttlinkedproduct_kernel(tc, query, keys_words, keys_scales, dquery, slot_factor, vals, offs2, offs, out):
     nc = tc.nc
     with ExitStack() as ctx:
         sb = ctx.enter_context(tc.tile_pool(name="sb", bufs=1))
-        reuse = ctx.enter_context(tc.tile_pool(name="reuse", bufs=1))
+        placed = ctx.enter_context(tc.tile_pool(name="placed", bufs=1))
         ps = ctx.enter_context(tc.psum_pool(name="ps", bufs=1))
 
         offs_t = sb.tile([P, LIST_COLS], U16, name="offs_t")
         offs2_t = sb.tile([P, LIST_COLS], U16, name="offs2_t")
-        kw = sb.tile([P, T], U16, name="kw")
-        ks = sb.tile([P, T], U8, name="ks")
+        key_words = sb.tile([P, T], U16, name="key_words")
+        key_scales = sb.tile([P, T], U8, name="key_scales")
         q_raw = [sb.tile([P, PACK, Q], F32, name="q_raw%d" % n) for n in range(2)]
-        os4 = sb.tile([P, PACK], F32, name="os4")
-        v_raw = [reuse.tile([P, T], F32, name="v_raw0", offset=0)] + [sb.tile([P, T], F32, name="v_raw%d" % j, tag="v_raw%d" % j, align_bytes=64) for j in range(1, 4)]
+        factor = sb.tile([P, PACK], F32, name="factor")
+        v_raw = [
+            placed.tile([P, T], F32, name="v_raw0", offset=0),
+            sb.tile([P, T], F32, name="v_raw1"),
+            sb.tile([P, T], F32, name="v_raw2"),
+            placed.tile([P, T], F32, name="v_raw3", offset=POOL_BYTES),
+        ]
         ident = sb.tile([P, P], F32, name="ident")
 
-
-        nc.gpsimd.memset(ks[:].bitcast(I32), 0)
+        nc.gpsimd.memset(key_scales[:].bitcast(I32), 0)
         make_identity(nc, ident[:])
 
         nc.sync.dma_start(offs_t[:], offs)
         nc.sync.dma_start(offs2_t[:], offs2)
-        nc.sync.dma_start(kw[:].bitcast(I32), keys_words[0].bitcast(I32))
+        nc.sync.dma_start(key_words[:].bitcast(I32), keys_words[0].bitcast(I32))
         nc.sync.dma_start(q_raw[0][:], query.rearrange("(p j) w -> p j w", j=PACK))
-        for r in range(4):
-            nc.sync.dma_start(ks[r:P:32, :].bitcast(I32), keys_scales[0, r:16:4, :].bitcast(I32))
+        for r in range(PACK):
+            nc.sync.dma_start(key_scales[r:P:QUADRANT, :].bitcast(I32), keys_scales[0, r : D // 32 : PACK, :].bitcast(I32))
         nc.sync.dma_start(q_raw[1][:], dquery.rearrange("(p j) w -> p j w", j=PACK))
         nc.sync.dma_start(v_raw[0][:], vals[0:P, :])
-        nc.sync.dma_start(os4[:], slot_factor.rearrange("o (p t) -> (o p) t", t=PACK))
-        for j in range(1, 4):
+        nc.sync.dma_start(factor[:], slot_factor.rearrange("o (p t) -> (o p) t", t=PACK))
+        for j in range(1, VALUE_TILES):
             nc.sync.dma_start(v_raw[j][:], vals[j * P : (j + 1) * P, :])
 
-        h = LIST_COLS // 2
-        halves = [(slice(s * HALF, (s + 1) * HALF), slice(s * h, (s + 1) * h)) for s in range(2)]
+        halves = [(slice(s * HALF, (s + 1) * HALF), slice(s * LIST_COLS // 2, (s + 1) * LIST_COLS // 2)) for s in range(2)]
 
         def wide(name):
             return sb.tile([P, SLOTS], F32, name=name)
@@ -64,108 +73,121 @@ def tile_attend_ttlinkedproduct_kernel(tc, query, keys_words, keys_scales, dquer
         def column(name):
             return sb.tile([P, 1], F32, name=name)
 
-        def quantise(grouped, codes, plane):
-            nc.vector.quantize_mx(out=codes.bitcast(FP8X4), scales=plane, in_=grouped.rearrange("p w j -> p (w j)"))
+        def quantise(grouped, codes, scales):
+            nc.vector.quantize_mx(out=codes.bitcast(FP8X4), scales=scales, in_=grouped.rearrange("p w j -> p (w j)"))
 
-        def product(acc, codes, plane, moving, moving_plane):
-            nc.tensor.matmul_mx(out=acc, lhsT=codes.bitcast(FP8X4), lhsT_scale=plane, rhs=moving, rhs_scale=moving_plane,
+        def product(acc, codes, scales, moving, moving_scales):
+            nc.tensor.matmul_mx(out=acc, lhsT=codes.bitcast(FP8X4), lhsT_scale=scales, rhs=moving, rhs_scale=moving_scales,
                                 start=True, stop=True)
 
-        kwg = sb.tile([P, SLOTS], U16, name="kwg", align_bytes=64)
-        ksg = [sb.tile([P, HALF], U8, name="ksg%d" % s, align_bytes=64) for s in range(2)]
+        listed_words = sb.tile([P, SLOTS], U16, name="listed_words", align_bytes=64)
+        listed_scales = [sb.tile([P, HALF], U8, name="listed_scales%d" % s, align_bytes=64) for s in range(2)]
         q_grouped = [sb.tile([P, Q, PACK], BF16, name="q_grouped%d" % n, align_bytes=64) for n in range(2)]
         q_codes = [sb.tile([P, Q], U32, name="q_codes%d" % n, align_bytes=64) for n in range(2)]
-        q_plane = [sb.tile([P, Q], U8, name="q_plane%d" % n, align_bytes=64) for n in range(2)]
+        q_scales = [sb.tile([P, Q], U8, name="q_scales%d" % n, align_bytes=64) for n in range(2)]
         a = ps.tile([P, SLOTS], F32, name="a", tag="bank_a")
         ta = ps.tile([P, SLOTS], F32, name="ta", tag="bank_ta")
 
-        nc.vector.tensor_copy(kwg[:], kw[:].indirect(offs_t[:]))
+        nc.vector.tensor_copy(listed_words[:], key_words[:].indirect(offs_t[:]))
         for n in range(2):
             nc.scalar.copy(q_grouped[n][:], q_raw[n][:].rearrange("p j w -> p w j"))
-        quantise(q_grouped[0][:], q_codes[0][:], q_plane[0][:])
+        quantise(q_grouped[0][:], q_codes[0][:], q_scales[0][:])
         for s, (cols, entries) in enumerate(halves):
-            nc.vector.tensor_copy(ksg[s][:], ks[:].indirect(offs_t[:, entries]))
-            product(a[:, cols], q_codes[0][:], q_plane[0][:], kwg[:, cols].bitcast(FP4X4), ksg[s][:])
-        quantise(q_grouped[1][:], q_codes[1][:], q_plane[1][:])
+            nc.vector.tensor_copy(listed_scales[s][:], key_scales[:].indirect(offs_t[:, entries]))
+            product(a[:, cols], q_codes[0][:], q_scales[0][:], listed_words[:, cols].bitcast(FP4X4), listed_scales[s][:])
+        quantise(q_grouped[1][:], q_codes[1][:], q_scales[1][:])
         for s, (cols, entries) in enumerate(halves):
-            product(ta[:, cols], q_codes[1][:], q_plane[1][:], kwg[:, cols].bitcast(FP4X4), ksg[s][:])
+            product(ta[:, cols], q_codes[1][:], q_scales[1][:], listed_words[:, cols].bitcast(FP4X4), listed_scales[s][:])
 
-        os_rows = ps.tile([P, PACK, P], F32, name="os_rows")
+        factor_rows = ps.tile([P, PACK, P], F32, name="factor_rows")
         for t in range(PACK):
-            nc.tensor.transpose(os_rows[:, t, :], os4[:, t : t + 1].to_broadcast([P, P]), ident[:])
+            nc.tensor.transpose(factor_rows[:, t, :], factor[:, t : t + 1].to_broadcast([P, P]), ident[:])
 
-        v_plane = [sb.tile([P, HALF], U8, name="v_plane%d" % s, align_bytes=64) for s in range(2)]
-        picked = [sb.tile([P, SLOTS], BF16, name="v_picked%d" % j) for j in range(4)]
+        def turn(listed, name, bank):
+            words = listed[:].bitcast(F32)
+            turned = ps.tile([P, 2, P], F32, name=name, tag=bank)
+            for u in range(2):
+                nc.tensor.transpose(turned[:, u, :], words[:, u:HALF:2], ident[:])
+            return turned
 
         def weave(copy, turned, grouped):
             copy(grouped.bitcast(F32), turned[:].rearrange("p u r -> p r u"))
 
-        def turn(j, bank):
-            words = picked[j][:].bitcast(F32)
-            turned = ps.tile([P, 2, P], F32, name="v%d_turned" % j, tag=bank)
-            for u in range(2):
-                nc.tensor.transpose(turned[:, u, :], words[:, u : HALF : 2], ident[:])
-            return turned
+        def look_up(linked, table):
+            for cols, entries in halves:
+                nc.scalar.activation(linked[:, cols], table[:].indirect(offs2_t[:, entries]), ACT.Copy)
 
-        nc.vector.tensor_copy(picked[0][:], v_raw[0][:].indirect(offs_t[:]))
-        pb, pb_sum = wide("pb"), column("pb_sum")
+        v0_listed = sb.tile([P, SLOTS], BF16, name="v0_listed")
+        nc.vector.tensor_copy(v0_listed[:], v_raw[0][:].indirect(offs_t[:]))
+
+        pb, pb_sum = sb.tile([P, SLOTS], F32, name="pb", tag="pb"), column("pb_sum")
         nc.scalar.activation(pb[:], a[:], ACT.Exp, scale=0.5, accum_out=pb_sum[:])
-
-        norm = reuse.tile([P, 1], F32, name="norm", offset=ROW_BYTES)
+        norm = placed.tile([P, 1], F32, name="norm", offset=ROW_BYTES)
         nc.vector.reciprocal(norm[:], pb_sum[:])
-        tpb = reuse.tile([P, SLOTS], F32, name="tpb", offset=0)
+        tpb = placed.tile([P, SLOTS], F32, name="tpb", offset=0)
         nc.vector.scalar_tensor_tensor(tpb[:], ta[:], 0.5, pb[:], ALU.mult, ALU.mult)
         pa = wide("pa")
-        nc.scalar.activation(pa[:], pb[:], ACT.Square, scale=norm[:])
-        pb_linked = reuse.tile([P, SLOTS], F32, name="pb_linked", offset=ROW_BYTES)
-        for cols, entries in halves:
-            nc.scalar.activation(pb_linked[:, cols], pb[:].indirect(offs2_t[:, entries]), ACT.Copy)
-        early_grouped = sb.tile([P, 2 * P, PACK], BF16, name="early_grouped", align_bytes=64)
-        weave(nc.scalar.copy, turn(0, "bank_v"), early_grouped[:, :P, :])
-        for j in range(1, 4):
-            nc.scalar.activation(picked[j][:], v_raw[j][:].indirect(offs_t[:]), ACT.Copy)
+        nc.vector.scalar_tensor_tensor(pa[:], pb[:], norm[:], pb[:], ALU.mult, ALU.mult)
 
-        linked = wide("linked")
-        for cols, entries in halves:
-            nc.vector.tensor_tensor(linked[:, cols], tpb[:].indirect(offs2_t[:, entries]), pa[:, cols], ALU.mult)
-        p, z = wide("p"), column("z")
-        nc.vector.scalar_tensor_tensor(p[:], pb_linked[:], 1.0, pa[:], ALU.mult, ALU.mult, accum_out=z[:])
+        pb_linked = wide("pb_linked")
+        look_up(pb_linked, pb)
+        tpb_linked = sb.tile([P, SLOTS], F32, name="tpb_linked", tag="pb")
+        look_up(tpb_linked, tpb)
+        v1_listed = placed.tile([P, SLOTS], BF16, name="v1_listed", offset=0)
+        v2_listed = sb.tile([P, SLOTS], BF16, name="v2_listed")
+        v3_listed = sb.tile([P, SLOTS], BF16, name="v3_listed")
+        nc.scalar.activation(v1_listed[:], v_raw[1][:].indirect(offs_t[:]), ACT.Copy)
+        nc.scalar.activation(v2_listed[:], v_raw[2][:].indirect(offs_t[:]), ACT.Copy)
+        nc.scalar.activation(v3_listed[:, : 16 * SCALAR_COLS], v_raw[LAST][:].indirect(offs_t[:, :SCALAR_COLS]), ACT.Copy)
+
+        v_codes = sb.tile([P, E], U32, name="v_codes", align_bytes=64)
+        v_scales = sb.tile([P, E], U8, name="v_scales", align_bytes=64)
+        v0_grouped = sb.tile([P, P, PACK], BF16, name="v0_grouped", align_bytes=64)
+        weave(nc.vector.tensor_copy, turn(v0_listed, "v0_turned", "bank_v"), v0_grouped[:])
+
+        p, z = wide("p"), sb.tile([P, 1], F32, name="z", tag="z")
+        nc.vector.scalar_tensor_tensor(p[:], pb_linked[:], norm[:], pa[:], ALU.mult, ALU.mult, accum_out=z[:])
         inv_z = column("inv_z")
         nc.vector.reciprocal(inv_z[:], z[:])
         own = wide("own")
         nc.vector.tensor_tensor(own[:], ta[:], p[:], ALU.mult)
+        linked = sb.tile([P, SLOTS], F32, name="linked", tag="z")
+        nc.vector.scalar_tensor_tensor(linked[:], tpb_linked[:], norm[:], pa[:], ALU.mult, ALU.mult)
         tp, tz = wide("tp"), column("tz")
         nc.vector.scalar_tensor_tensor(tp[:], own[:], 1.0, linked[:], ALU.mult, ALU.add, accum_out=tz[:])
-        weave(nc.vector.tensor_copy, turn(1, "bank_ta"), early_grouped[:, P:, :])
+        quantise(v0_grouped[:], v_codes[:, :P], v_scales[:, :P])
         neg_ratio = column("neg_ratio")
         nc.vector.tensor_scalar(neg_ratio[:], tz[:], inv_z[:], -1.0, ALU.mult, ALU.mult)
-        centred = sb.tile([P, SLOTS], F32, name="centred", tag="centred", align_bytes=64)
+        centred = wide("centred")
         nc.vector.scalar_tensor_tensor(centred[:], p[:], neg_ratio[:], tp[:], ALU.mult, ALU.add)
-
+        v1_turned = turn(v1_listed, "v1_turned", "bank_ta")
+        v2_turned = turn(v2_listed, "v2_turned", "bank_v")
         w = sb.tile([P, 2, P, 2], BF16, name="w")
         w_turned = ps.tile([P, 2, P], F32, name="w_turned")
         by_place = centred[:].rearrange("q (s t) -> q s t", t=PACK)
-        v2_turned = turn(2, "bank_v")
         for u in range(2):
-            nc.vector.scalar_tensor_tensor(w[:, u, :, :], by_place[:, :, 2 * u : 2 * u + 2], inv_z[:],
-                                           os_rows[:, 2 * u : 2 * u + 2, :].rearrange("q t s -> q s t"), ALU.mult, ALU.mult)
+            places = slice(2 * u, 2 * u + 2)
+            nc.vector.scalar_tensor_tensor(w[:, u, :, :], by_place[:, :, places], inv_z[:],
+                                           factor_rows[:, places, :].rearrange("q t s -> q s t"), ALU.mult, ALU.mult)
             nc.tensor.transpose(w_turned[:, u, :], w[:, u, :, :].rearrange("q s e -> q (s e)").bitcast(F32), ident[:])
-        v_codes = [sb.tile([P, HALF], U32, name="v_codes%d" % s, tag=("centred", "late_codes")[s], align_bytes=64) for s in range(2)]
-        quantise(early_grouped[:], v_codes[0][:], v_plane[0][:])
-        late_grouped = sb.tile([P, 2 * P, PACK], BF16, name="late_grouped", tag="v_raw3", align_bytes=64)
-        weave(nc.scalar.copy, v2_turned, late_grouped[:, :P, :])
-        w_grouped = sb.tile([P, P, PACK], BF16, name="w_grouped", align_bytes=64)
+        nc.vector.tensor_copy(v3_listed[:, 16 * SCALAR_COLS :], v_raw[LAST][:].indirect(offs_t[:, SCALAR_COLS:]))
+
+        w_grouped = placed.tile([P, Q, PACK], BF16, name="w_grouped", offset=POOL_BYTES, align_bytes=64)
+        rest_grouped = placed.tile([P, LAST * P, PACK], BF16, name="rest_grouped", offset=POOL_BYTES + GROUPED_BYTES, align_bytes=64)
         weave(nc.vector.tensor_copy, w_turned, w_grouped[:])
+        weave(nc.scalar.copy, v1_turned, rest_grouped[:, :P, :])
+        weave(nc.scalar.copy, v2_turned, rest_grouped[:, P : 2 * P, :])
+        weave(nc.scalar.copy, turn(v3_listed, "v3_turned", "bank_a"), rest_grouped[:, 2 * P :, :])
         w_codes = sb.tile([P, Q], U32, name="w_codes", align_bytes=64)
-        w_plane = sb.tile([P, Q], U8, name="w_plane", align_bytes=64)
-        quantise(w_grouped[:], w_codes[:], w_plane[:])
-        weave(nc.scalar.copy, turn(3, "bank_a"), late_grouped[:, P:, :])
-        quantise(late_grouped[:], v_codes[1][:], v_plane[1][:])
+        w_scales = sb.tile([P, Q], U8, name="w_scales", align_bytes=64)
+        quantise(w_grouped[:], w_codes[:], w_scales[:])
+        quantise(rest_grouped[:, : 2 * P, :], v_codes[:, P : LAST * P], v_scales[:, P : LAST * P])
+        quantise(rest_grouped[:, 2 * P :, :], v_codes[:, LAST * P :], v_scales[:, LAST * P :])
 
         result = sb.tile([P, E], F32, name="result")
-        for s, (bank, copy, queue) in enumerate((("bank_a", nc.scalar.copy, nc.scalar), ("bank_late", nc.vector.tensor_copy, nc.sync))):
-            cols = halves[s][0]
-            acc = ps.tile([P, HALF], F32, name="acc%d" % s, tag=bank)
-            product(acc[:], w_codes[:], w_plane[:], v_codes[s][:].bitcast(FP8X4), v_plane[s][:])
-            copy(result[:, cols], acc[:])
-            queue.dma_start(out[:, cols], result[:, cols])
+        for s, (bank, copy, queue) in enumerate((("bank_a", nc.scalar.copy, nc.scalar), ("bank_out", nc.vector.tensor_copy, nc.sync))):
+            features = slice(s * E // 2, (s + 1) * E // 2)
+            acc = ps.tile([P, E // 2], F32, name="acc%d" % s, tag=bank)
+            product(acc[:], w_codes[:], w_scales[:], v_codes[:, features].bitcast(FP8X4), v_scales[:, features])
+            copy(result[:, features], acc[:])
+            queue.dma_start(out[:, features], result[:, features])

@@ -23,10 +23,7 @@ VALUE_TILES = E // P
 LAST = VALUE_TILES - 1
 LIST_COLS = SLOTS // 16
 HALF = SLOTS // 2
-POOL_BYTES = 4 * T
 ROW_BYTES = 4 * SLOTS
-GROUPED_BYTES = 2 * P * PACK
-SCALAR_COLS = 22
 
 
 def tile_attend_ttlinkedproduct_kernel(tc, query, keys_words, keys_scales, dquery, slot_factor, vals, offs2, offs, out):
@@ -42,11 +39,8 @@ def tile_attend_ttlinkedproduct_kernel(tc, query, keys_words, keys_scales, dquer
         key_scales = sb.tile([P, T], U8, name="key_scales")
         q_raw = [sb.tile([P, PACK, Q], F32, name="q_raw%d" % n) for n in range(2)]
         factor = sb.tile([P, PACK], F32, name="factor")
-        v_raw = [
-            placed.tile([P, T], F32, name="v_raw0", offset=0),
-            sb.tile([P, T], F32, name="v_raw1"),
-            sb.tile([P, T], F32, name="v_raw2"),
-            placed.tile([P, T], F32, name="v_raw3", offset=POOL_BYTES),
+        v_raw = [placed.tile([P, T], F32, name="v_raw0", offset=0)] + [
+            sb.tile([P, T], F32, name="v_raw%d" % j, tag="v_raw%d" % j, align_bytes=64) for j in range(1, VALUE_TILES)
         ]
         ident = sb.tile([P, P], F32, name="ident")
 
@@ -85,7 +79,7 @@ def tile_attend_ttlinkedproduct_kernel(tc, query, keys_words, keys_scales, dquer
         q_grouped = [sb.tile([P, Q, PACK], BF16, name="q_grouped%d" % n, align_bytes=64) for n in range(2)]
         q_codes = [sb.tile([P, Q], U32, name="q_codes%d" % n, align_bytes=64) for n in range(2)]
         q_scales = [sb.tile([P, Q], U8, name="q_scales%d" % n, align_bytes=64) for n in range(2)]
-        a = ps.tile([P, SLOTS], F32, name="a", tag="bank_a")
+        a = [ps.tile([P, HALF], F32, name="a%d" % s, tag="bank_a%d" % s) for s in range(2)]
         ta = ps.tile([P, SLOTS], F32, name="ta", tag="bank_ta")
 
         nc.vector.tensor_copy(listed_words[:], key_words[:].indirect(offs_t[:]))
@@ -94,7 +88,7 @@ def tile_attend_ttlinkedproduct_kernel(tc, query, keys_words, keys_scales, dquer
         quantise(q_grouped[0][:], q_codes[0][:], q_scales[0][:])
         for s, (cols, entries) in enumerate(halves):
             nc.vector.tensor_copy(listed_scales[s][:], key_scales[:].indirect(offs_t[:, entries]))
-            product(a[:, cols], q_codes[0][:], q_scales[0][:], listed_words[:, cols].bitcast(FP4X4), listed_scales[s][:])
+            product(a[s][:], q_codes[0][:], q_scales[0][:], listed_words[:, cols].bitcast(FP4X4), listed_scales[s][:])
         quantise(q_grouped[1][:], q_codes[1][:], q_scales[1][:])
         for s, (cols, entries) in enumerate(halves):
             product(ta[:, cols], q_codes[1][:], q_scales[1][:], listed_words[:, cols].bitcast(FP4X4), listed_scales[s][:])
@@ -120,28 +114,30 @@ def tile_attend_ttlinkedproduct_kernel(tc, query, keys_words, keys_scales, dquer
         v0_listed = sb.tile([P, SLOTS], BF16, name="v0_listed")
         nc.vector.tensor_copy(v0_listed[:], v_raw[0][:].indirect(offs_t[:]))
 
-        pb, pb_sum = sb.tile([P, SLOTS], F32, name="pb", tag="pb"), column("pb_sum")
-        nc.scalar.activation(pb[:], a[:], ACT.Exp, scale=0.5, accum_out=pb_sum[:])
-        norm = placed.tile([P, 1], F32, name="norm", offset=ROW_BYTES)
-        nc.vector.reciprocal(norm[:], pb_sum[:])
+        pb = wide("pb")
+        pb_sums = [column("pb_sum%d" % s) for s in range(2)]
+        for s, (cols, entries) in enumerate(halves):
+            nc.scalar.activation(pb[:, cols], a[s][:], ACT.Exp, scale=0.5, accum_out=pb_sums[s][:])
+        pb_sum = placed.tile([P, 1], F32, name="pb_sum", offset=ROW_BYTES)
+        nc.vector.tensor_tensor(pb_sum[:], pb_sums[0][:], pb_sums[1][:], ALU.add)
         tpb = placed.tile([P, SLOTS], F32, name="tpb", offset=0)
         nc.vector.scalar_tensor_tensor(tpb[:], ta[:], 0.5, pb[:], ALU.mult, ALU.mult)
+        norm = column("norm")
+        nc.vector.reciprocal(norm[:], pb_sum[:])
         pa = wide("pa")
         nc.vector.scalar_tensor_tensor(pa[:], pb[:], norm[:], pb[:], ALU.mult, ALU.mult)
 
         pb_linked = wide("pb_linked")
         look_up(pb_linked, pb)
-        tpb_linked = sb.tile([P, SLOTS], F32, name="tpb_linked", tag="pb")
+        tpb_linked = wide("tpb_linked")
         look_up(tpb_linked, tpb)
         v1_listed = placed.tile([P, SLOTS], BF16, name="v1_listed", offset=0)
         v2_listed = sb.tile([P, SLOTS], BF16, name="v2_listed")
         v3_listed = sb.tile([P, SLOTS], BF16, name="v3_listed")
         nc.scalar.activation(v1_listed[:], v_raw[1][:].indirect(offs_t[:]), ACT.Copy)
         nc.scalar.activation(v2_listed[:], v_raw[2][:].indirect(offs_t[:]), ACT.Copy)
-        nc.scalar.activation(v3_listed[:, : 16 * SCALAR_COLS], v_raw[LAST][:].indirect(offs_t[:, :SCALAR_COLS]), ACT.Copy)
+        middle_grouped = sb.tile([P, 2 * P, PACK], BF16, name="middle_grouped", tag="v_raw2", align_bytes=64)
 
-        v_codes = sb.tile([P, E], U32, name="v_codes", align_bytes=64)
-        v_scales = sb.tile([P, E], U8, name="v_scales", align_bytes=64)
         v0_grouped = sb.tile([P, P, PACK], BF16, name="v0_grouped", align_bytes=64)
         weave(nc.vector.tensor_copy, turn(v0_listed, "v0_turned", "bank_v"), v0_grouped[:])
 
@@ -155,13 +151,13 @@ def tile_attend_ttlinkedproduct_kernel(tc, query, keys_words, keys_scales, dquer
         nc.vector.scalar_tensor_tensor(linked[:], tpb_linked[:], norm[:], pa[:], ALU.mult, ALU.mult)
         tp, tz = wide("tp"), column("tz")
         nc.vector.scalar_tensor_tensor(tp[:], own[:], 1.0, linked[:], ALU.mult, ALU.add, accum_out=tz[:])
-        quantise(v0_grouped[:], v_codes[:, :P], v_scales[:, :P])
         neg_ratio = column("neg_ratio")
         nc.vector.tensor_scalar(neg_ratio[:], tz[:], inv_z[:], -1.0, ALU.mult, ALU.mult)
-        centred = wide("centred")
+        centred = sb.tile([P, SLOTS], F32, name="centred", tag="centred", align_bytes=64)
         nc.vector.scalar_tensor_tensor(centred[:], p[:], neg_ratio[:], tp[:], ALU.mult, ALU.add)
-        v1_turned = turn(v1_listed, "v1_turned", "bank_ta")
-        v2_turned = turn(v2_listed, "v2_turned", "bank_v")
+        weave(nc.scalar.copy, turn(v1_listed, "v1_turned", "bank_ta"), middle_grouped[:, :P, :])
+        weave(nc.scalar.copy, turn(v2_listed, "v2_turned", "bank_v"), middle_grouped[:, P:, :])
+        nc.scalar.activation(v3_listed[:], v_raw[LAST][:].indirect(offs_t[:]), ACT.Copy)
         w = sb.tile([P, 2, P, 2], BF16, name="w")
         w_turned = ps.tile([P, 2, P], F32, name="w_turned")
         by_place = centred[:].rearrange("q (s t) -> q s t", t=PACK)
@@ -170,22 +166,22 @@ def tile_attend_ttlinkedproduct_kernel(tc, query, keys_words, keys_scales, dquer
             nc.vector.scalar_tensor_tensor(w[:, u, :, :], by_place[:, :, places], inv_z[:],
                                            factor_rows[:, places, :].rearrange("q t s -> q s t"), ALU.mult, ALU.mult)
             nc.tensor.transpose(w_turned[:, u, :], w[:, u, :, :].rearrange("q s e -> q (s e)").bitcast(F32), ident[:])
-        nc.vector.tensor_copy(v3_listed[:, 16 * SCALAR_COLS :], v_raw[LAST][:].indirect(offs_t[:, SCALAR_COLS:]))
 
-        w_grouped = placed.tile([P, Q, PACK], BF16, name="w_grouped", offset=POOL_BYTES, align_bytes=64)
-        rest_grouped = placed.tile([P, LAST * P, PACK], BF16, name="rest_grouped", offset=POOL_BYTES + GROUPED_BYTES, align_bytes=64)
+        v_codes = sb.tile([P, E], U32, name="v_codes", tag="centred", align_bytes=64)
+        v_scales = sb.tile([P, E], U8, name="v_scales", align_bytes=64)
+        quantise(v0_grouped[:], v_codes[:, :P], v_scales[:, :P])
+        quantise(middle_grouped[:], v_codes[:, P : LAST * P], v_scales[:, P : LAST * P])
+        w_grouped = sb.tile([P, Q, PACK], BF16, name="w_grouped", align_bytes=64)
         weave(nc.vector.tensor_copy, w_turned, w_grouped[:])
-        weave(nc.scalar.copy, v1_turned, rest_grouped[:, :P, :])
-        weave(nc.scalar.copy, v2_turned, rest_grouped[:, P : 2 * P, :])
-        weave(nc.scalar.copy, turn(v3_listed, "v3_turned", "bank_a"), rest_grouped[:, 2 * P :, :])
         w_codes = sb.tile([P, Q], U32, name="w_codes", align_bytes=64)
         w_scales = sb.tile([P, Q], U8, name="w_scales", align_bytes=64)
         quantise(w_grouped[:], w_codes[:], w_scales[:])
-        quantise(rest_grouped[:, : 2 * P, :], v_codes[:, P : LAST * P], v_scales[:, P : LAST * P])
-        quantise(rest_grouped[:, 2 * P :, :], v_codes[:, LAST * P :], v_scales[:, LAST * P :])
+        v3_grouped = sb.tile([P, P, PACK], BF16, name="v3_grouped", align_bytes=64)
+        weave(nc.scalar.copy, turn(v3_listed, "v3_turned", "bank_a0"), v3_grouped[:])
+        quantise(v3_grouped[:], v_codes[:, LAST * P :], v_scales[:, LAST * P :])
 
         result = sb.tile([P, E], F32, name="result")
-        for s, (bank, copy, queue) in enumerate((("bank_a", nc.scalar.copy, nc.scalar), ("bank_out", nc.vector.tensor_copy, nc.sync))):
+        for s, (bank, copy, queue) in enumerate((("bank_a0", nc.scalar.copy, nc.scalar), ("bank_a1", nc.vector.tensor_copy, nc.sync))):
             features = slice(s * E // 2, (s + 1) * E // 2)
             acc = ps.tile([P, E // 2], F32, name="acc%d" % s, tag=bank)
             product(acc[:], w_codes[:], w_scales[:], v_codes[:, features].bitcast(FP8X4), v_scales[:, features])

@@ -23,7 +23,9 @@ VALUE_TILES = E // P
 LAST = VALUE_TILES - 1
 LIST_COLS = SLOTS // 16
 HALF = SLOTS // 2
+POOL_BYTES = 4 * T
 ROW_BYTES = 4 * SLOTS
+SCALAR_COLS = 22
 
 
 def tile_attend_ttlinkedproduct_kernel(tc, query, keys_words, keys_scales, dquery, slot_factor, vals, offs2, offs, out):
@@ -39,8 +41,11 @@ def tile_attend_ttlinkedproduct_kernel(tc, query, keys_words, keys_scales, dquer
         key_scales = sb.tile([P, T], U8, name="key_scales")
         q_raw = [sb.tile([P, PACK, Q], F32, name="q_raw%d" % n) for n in range(2)]
         factor = sb.tile([P, PACK], F32, name="factor")
-        v_raw = [placed.tile([P, T], F32, name="v_raw0", offset=0)] + [
-            sb.tile([P, T], F32, name="v_raw%d" % j, tag="v_raw%d" % j, align_bytes=64) for j in range(1, VALUE_TILES)
+        v_raw = [
+            placed.tile([P, T], F32, name="v_raw0", offset=0),
+            sb.tile([P, T], F32, name="v_raw1"),
+            sb.tile([P, T], F32, name="v_raw2", tag="v_raw2", align_bytes=64),
+            placed.tile([P, T], F32, name="v_raw3", offset=POOL_BYTES),
         ]
         ident = sb.tile([P, P], F32, name="ident")
 
@@ -151,13 +156,16 @@ def tile_attend_ttlinkedproduct_kernel(tc, query, keys_words, keys_scales, dquer
         nc.vector.scalar_tensor_tensor(linked[:], tpb_linked[:], norm[:], pa[:], ALU.mult, ALU.mult)
         tp, tz = wide("tp"), column("tz")
         nc.vector.scalar_tensor_tensor(tp[:], own[:], 1.0, linked[:], ALU.mult, ALU.add, accum_out=tz[:])
+        outer_codes = sb.tile([P, 2 * P], U32, name="outer_codes", align_bytes=64)
+        outer_scales = sb.tile([P, 2 * P], U8, name="outer_scales", align_bytes=64)
+        quantise(v0_grouped[:], outer_codes[:, :P], outer_scales[:, :P])
         neg_ratio = column("neg_ratio")
         nc.vector.tensor_scalar(neg_ratio[:], tz[:], inv_z[:], -1.0, ALU.mult, ALU.mult)
-        centred = sb.tile([P, SLOTS], F32, name="centred", tag="centred", align_bytes=64)
+        centred = wide("centred")
         nc.vector.scalar_tensor_tensor(centred[:], p[:], neg_ratio[:], tp[:], ALU.mult, ALU.add)
         weave(nc.scalar.copy, turn(v1_listed, "v1_turned", "bank_ta"), middle_grouped[:, :P, :])
         weave(nc.scalar.copy, turn(v2_listed, "v2_turned", "bank_v"), middle_grouped[:, P:, :])
-        nc.scalar.activation(v3_listed[:], v_raw[LAST][:].indirect(offs_t[:]), ACT.Copy)
+        nc.scalar.activation(v3_listed[:, : 16 * SCALAR_COLS], v_raw[LAST][:].indirect(offs_t[:, :SCALAR_COLS]), ACT.Copy)
         w = sb.tile([P, 2, P, 2], BF16, name="w")
         w_turned = ps.tile([P, 2, P], F32, name="w_turned")
         by_place = centred[:].rearrange("q (s t) -> q s t", t=PACK)
@@ -166,24 +174,27 @@ def tile_attend_ttlinkedproduct_kernel(tc, query, keys_words, keys_scales, dquer
             nc.vector.scalar_tensor_tensor(w[:, u, :, :], by_place[:, :, places], inv_z[:],
                                            factor_rows[:, places, :].rearrange("q t s -> q s t"), ALU.mult, ALU.mult)
             nc.tensor.transpose(w_turned[:, u, :], w[:, u, :, :].rearrange("q s e -> q (s e)").bitcast(F32), ident[:])
+        nc.vector.tensor_copy(v3_listed[:, 16 * SCALAR_COLS :], v_raw[LAST][:].indirect(offs_t[:, SCALAR_COLS:]))
 
-        v_codes = sb.tile([P, E], U32, name="v_codes", tag="centred", align_bytes=64)
-        v_scales = sb.tile([P, E], U8, name="v_scales", align_bytes=64)
-        quantise(v0_grouped[:], v_codes[:, :P], v_scales[:, :P])
-        quantise(middle_grouped[:], v_codes[:, P : LAST * P], v_scales[:, P : LAST * P])
-        w_grouped = sb.tile([P, Q, PACK], BF16, name="w_grouped", align_bytes=64)
+        w_grouped = placed.tile([P, Q, PACK], BF16, name="w_grouped", offset=POOL_BYTES, align_bytes=64)
         weave(nc.vector.tensor_copy, w_turned, w_grouped[:])
+        middle_codes = placed.tile([P, 2 * P], U32, name="middle_codes", offset=POOL_BYTES + ROW_BYTES, align_bytes=64)
+        middle_scales = sb.tile([P, 2 * P], U8, name="middle_scales", align_bytes=64)
+        quantise(middle_grouped[:], middle_codes[:], middle_scales[:])
         w_codes = sb.tile([P, Q], U32, name="w_codes", align_bytes=64)
         w_scales = sb.tile([P, Q], U8, name="w_scales", align_bytes=64)
         quantise(w_grouped[:], w_codes[:], w_scales[:])
         v3_grouped = sb.tile([P, P, PACK], BF16, name="v3_grouped", align_bytes=64)
         weave(nc.scalar.copy, turn(v3_listed, "v3_turned", "bank_a0"), v3_grouped[:])
-        quantise(v3_grouped[:], v_codes[:, LAST * P :], v_scales[:, LAST * P :])
+        quantise(v3_grouped[:], outer_codes[:, P:], outer_scales[:, P:])
 
-        result = sb.tile([P, E], F32, name="result")
-        for s, (bank, copy, queue) in enumerate((("bank_a0", nc.scalar.copy, nc.scalar), ("bank_a1", nc.vector.tensor_copy, nc.sync))):
-            features = slice(s * E // 2, (s + 1) * E // 2)
-            acc = ps.tile([P, E // 2], F32, name="acc%d" % s, tag=bank)
-            product(acc[:], w_codes[:], w_scales[:], v_codes[:, features].bitcast(FP8X4), v_scales[:, features])
-            copy(result[:, features], acc[:])
-            queue.dma_start(out[:, features], result[:, features])
+        out_tiles = out.rearrange("q (j e) -> q j e", e=P)
+        for codes, scales, tiles, bank, copy, queue in (
+            (middle_codes, middle_scales, slice(1, LAST), "bank_a0", nc.scalar.copy, nc.scalar),
+            (outer_codes, outer_scales, slice(0, VALUE_TILES, LAST), "bank_a1", nc.vector.tensor_copy, nc.sync),
+        ):
+            acc = ps.tile([P, 2 * P], F32, name="acc_" + bank, tag=bank)
+            product(acc[:], w_codes[:], w_scales[:], codes[:].bitcast(FP8X4), scales[:])
+            result = sb.tile([P, 2, P], F32, name="result_" + bank)
+            copy(result[:].rearrange("q j e -> q (j e)"), acc[:])
+            queue.dma_start(out_tiles[:, tiles, :], result[:])

from contextlib import ExitStack

import concourse.mybir as mybir
from concourse.masks import make_identity

F32 = mybir.dt.float32
BF16 = mybir.dt.bfloat16
I32 = mybir.dt.int32
U32 = mybir.dt.uint32
U16 = mybir.dt.uint16
U8 = mybir.dt.uint8
FP8X4 = mybir.dt.float8_e4m3fn_x4
FP4X4 = mybir.dt.float4_e2m1fn_x4
ALU = mybir.AluOpType
ACT = mybir.ActivationFunctionType

P = 128
PACK = 4
QUADRANT = 32
D, E, T, SLOTS, Q = 512, 512, 2048, 512, 128
FLOPS = 2 * (2 * D * Q * SLOTS) + 2 * SLOTS * Q * E
VALUE_TILES = E // P
LAST = VALUE_TILES - 1
LIST_COLS = SLOTS // 16
HALF = SLOTS // 2
POOL_BYTES = 4 * T
ROW_BYTES = 4 * SLOTS
SCALAR_COLS = 22


def tile_attend_ttlinkedproduct_kernel(tc, query, keys_words, keys_scales, dquery, slot_factor, vals, offs2, offs, out):
    nc = tc.nc
    with ExitStack() as ctx:
        sb = ctx.enter_context(tc.tile_pool(name="sb", bufs=1))
        placed = ctx.enter_context(tc.tile_pool(name="placed", bufs=1))
        ps = ctx.enter_context(tc.psum_pool(name="ps", bufs=1))

        offs_t = sb.tile([P, LIST_COLS], U16, name="offs_t")
        offs2_t = sb.tile([P, LIST_COLS], U16, name="offs2_t")
        key_words = sb.tile([P, T], U16, name="key_words")
        key_scales = sb.tile([P, T], U8, name="key_scales")
        q_raw = [sb.tile([P, PACK, Q], F32, name="q_raw%d" % n) for n in range(2)]
        factor = sb.tile([P, PACK], F32, name="factor")
        v_raw = [
            placed.tile([P, T], F32, name="v_raw0", offset=0),
            sb.tile([P, T], F32, name="v_raw1"),
            sb.tile([P, T], F32, name="v_raw2", tag="v_raw2", align_bytes=64),
            placed.tile([P, T], F32, name="v_raw3", offset=POOL_BYTES),
        ]
        ident = sb.tile([P, P], F32, name="ident")

        nc.gpsimd.memset(key_scales[:].bitcast(I32), 0)
        make_identity(nc, ident[:])

        nc.sync.dma_start(offs_t[:], offs)
        nc.sync.dma_start(offs2_t[:], offs2)
        nc.sync.dma_start(key_words[:].bitcast(I32), keys_words[0].bitcast(I32))
        nc.sync.dma_start(q_raw[0][:], query.rearrange("(p j) w -> p j w", j=PACK))
        for r in range(PACK):
            nc.sync.dma_start(key_scales[r:P:QUADRANT, :].bitcast(I32), keys_scales[0, r : D // 32 : PACK, :].bitcast(I32))
        nc.sync.dma_start(q_raw[1][:], dquery.rearrange("(p j) w -> p j w", j=PACK))
        nc.sync.dma_start(v_raw[0][:], vals[0:P, :])
        nc.sync.dma_start(factor[:], slot_factor.rearrange("o (p t) -> (o p) t", t=PACK))
        for j in range(1, VALUE_TILES):
            nc.sync.dma_start(v_raw[j][:], vals[j * P : (j + 1) * P, :])

        halves = [(slice(s * HALF, (s + 1) * HALF), slice(s * LIST_COLS // 2, (s + 1) * LIST_COLS // 2)) for s in range(2)]

        def wide(name):
            return sb.tile([P, SLOTS], F32, name=name)

        def column(name):
            return sb.tile([P, 1], F32, name=name)

        def quantise(grouped, codes, scales):
            nc.vector.quantize_mx(out=codes.bitcast(FP8X4), scales=scales, in_=grouped.rearrange("p w j -> p (w j)"))

        def product(acc, codes, scales, moving, moving_scales):
            nc.tensor.matmul_mx(out=acc, lhsT=codes.bitcast(FP8X4), lhsT_scale=scales, rhs=moving, rhs_scale=moving_scales,
                                start=True, stop=True)

        listed_words = sb.tile([P, SLOTS], U16, name="listed_words", align_bytes=64)
        listed_scales = [sb.tile([P, HALF], U8, name="listed_scales%d" % s, align_bytes=64) for s in range(2)]
        q_grouped = [sb.tile([P, Q, PACK], BF16, name="q_grouped%d" % n, align_bytes=64) for n in range(2)]
        q_codes = [sb.tile([P, Q], U32, name="q_codes%d" % n, align_bytes=64) for n in range(2)]
        q_scales = [sb.tile([P, Q], U8, name="q_scales%d" % n, align_bytes=64) for n in range(2)]
        a = [ps.tile([P, HALF], F32, name="a%d" % s, tag="bank_a%d" % s) for s in range(2)]
        ta = ps.tile([P, SLOTS], F32, name="ta", tag="bank_ta")

        nc.vector.tensor_copy(listed_words[:], key_words[:].indirect(offs_t[:]))
        for n in range(2):
            nc.scalar.copy(q_grouped[n][:], q_raw[n][:].rearrange("p j w -> p w j"))
        quantise(q_grouped[0][:], q_codes[0][:], q_scales[0][:])
        for s, (cols, entries) in enumerate(halves):
            nc.vector.tensor_copy(listed_scales[s][:], key_scales[:].indirect(offs_t[:, entries]))
            product(a[s][:], q_codes[0][:], q_scales[0][:], listed_words[:, cols].bitcast(FP4X4), listed_scales[s][:])
        quantise(q_grouped[1][:], q_codes[1][:], q_scales[1][:])
        for s, (cols, entries) in enumerate(halves):
            product(ta[:, cols], q_codes[1][:], q_scales[1][:], listed_words[:, cols].bitcast(FP4X4), listed_scales[s][:])

        factor_rows = ps.tile([P, PACK, P], F32, name="factor_rows")
        for t in range(PACK):
            nc.tensor.transpose(factor_rows[:, t, :], factor[:, t : t + 1].to_broadcast([P, P]), ident[:])

        def turn(listed, name, bank):
            words = listed[:].bitcast(F32)
            turned = ps.tile([P, 2, P], F32, name=name, tag=bank)
            for u in range(2):
                nc.tensor.transpose(turned[:, u, :], words[:, u:HALF:2], ident[:])
            return turned

        def weave(copy, turned, grouped):
            copy(grouped.bitcast(F32), turned[:].rearrange("p u r -> p r u"))

        def look_up(linked, table):
            for cols, entries in halves:
                nc.scalar.activation(linked[:, cols], table[:].indirect(offs2_t[:, entries]), ACT.Copy)

        v0_listed = sb.tile([P, SLOTS], BF16, name="v0_listed")
        nc.vector.tensor_copy(v0_listed[:], v_raw[0][:].indirect(offs_t[:]))

        pb = wide("pb")
        pb_sums = [column("pb_sum%d" % s) for s in range(2)]
        for s, (cols, entries) in enumerate(halves):
            nc.scalar.activation(pb[:, cols], a[s][:], ACT.Exp, scale=0.5, accum_out=pb_sums[s][:])
        pb_sum = placed.tile([P, 1], F32, name="pb_sum", offset=ROW_BYTES)
        nc.vector.tensor_tensor(pb_sum[:], pb_sums[0][:], pb_sums[1][:], ALU.add)
        tpb = placed.tile([P, SLOTS], F32, name="tpb", offset=0)
        nc.vector.scalar_tensor_tensor(tpb[:], ta[:], 0.5, pb[:], ALU.mult, ALU.mult)
        norm = column("norm")
        nc.vector.reciprocal(norm[:], pb_sum[:])
        pa = wide("pa")
        nc.vector.scalar_tensor_tensor(pa[:], pb[:], norm[:], pb[:], ALU.mult, ALU.mult)

        pb_linked = wide("pb_linked")
        look_up(pb_linked, pb)
        tpb_linked = wide("tpb_linked")
        look_up(tpb_linked, tpb)
        v1_listed = placed.tile([P, SLOTS], BF16, name="v1_listed", offset=0)
        v2_listed = sb.tile([P, SLOTS], BF16, name="v2_listed")
        v3_listed = sb.tile([P, SLOTS], BF16, name="v3_listed")
        nc.scalar.activation(v1_listed[:], v_raw[1][:].indirect(offs_t[:]), ACT.Copy)
        nc.scalar.activation(v2_listed[:], v_raw[2][:].indirect(offs_t[:]), ACT.Copy)
        middle_grouped = sb.tile([P, 2 * P, PACK], BF16, name="middle_grouped", tag="v_raw2", align_bytes=64)

        v0_grouped = sb.tile([P, P, PACK], BF16, name="v0_grouped", align_bytes=64)
        weave(nc.vector.tensor_copy, turn(v0_listed, "v0_turned", "bank_v"), v0_grouped[:])

        p, z = wide("p"), sb.tile([P, 1], F32, name="z", tag="z")
        nc.vector.scalar_tensor_tensor(p[:], pb_linked[:], norm[:], pa[:], ALU.mult, ALU.mult, accum_out=z[:])
        inv_z = column("inv_z")
        nc.vector.reciprocal(inv_z[:], z[:])
        own = wide("own")
        nc.vector.tensor_tensor(own[:], ta[:], p[:], ALU.mult)
        linked = sb.tile([P, SLOTS], F32, name="linked", tag="z")
        nc.vector.scalar_tensor_tensor(linked[:], tpb_linked[:], norm[:], pa[:], ALU.mult, ALU.mult)
        tp, tz = wide("tp"), column("tz")
        nc.vector.scalar_tensor_tensor(tp[:], own[:], 1.0, linked[:], ALU.mult, ALU.add, accum_out=tz[:])
        outer_codes = sb.tile([P, 2 * P], U32, name="outer_codes", align_bytes=64)
        outer_scales = sb.tile([P, 2 * P], U8, name="outer_scales", align_bytes=64)
        quantise(v0_grouped[:], outer_codes[:, :P], outer_scales[:, :P])
        neg_ratio = column("neg_ratio")
        nc.vector.tensor_scalar(neg_ratio[:], tz[:], inv_z[:], -1.0, ALU.mult, ALU.mult)
        centred = wide("centred")
        nc.vector.scalar_tensor_tensor(centred[:], p[:], neg_ratio[:], tp[:], ALU.mult, ALU.add)
        weave(nc.scalar.copy, turn(v1_listed, "v1_turned", "bank_ta"), middle_grouped[:, :P, :])
        weave(nc.scalar.copy, turn(v2_listed, "v2_turned", "bank_v"), middle_grouped[:, P:, :])
        nc.scalar.activation(v3_listed[:, : 16 * SCALAR_COLS], v_raw[LAST][:].indirect(offs_t[:, :SCALAR_COLS]), ACT.Copy)
        w = sb.tile([P, 2, P, 2], BF16, name="w")
        w_turned = ps.tile([P, 2, P], F32, name="w_turned")
        by_place = centred[:].rearrange("q (s t) -> q s t", t=PACK)
        for u in range(2):
            places = slice(2 * u, 2 * u + 2)
            nc.vector.scalar_tensor_tensor(w[:, u, :, :], by_place[:, :, places], inv_z[:],
                                           factor_rows[:, places, :].rearrange("q t s -> q s t"), ALU.mult, ALU.mult)
            nc.tensor.transpose(w_turned[:, u, :], w[:, u, :, :].rearrange("q s e -> q (s e)").bitcast(F32), ident[:])
        nc.vector.tensor_copy(v3_listed[:, 16 * SCALAR_COLS :], v_raw[LAST][:].indirect(offs_t[:, SCALAR_COLS:]))

        w_grouped = placed.tile([P, Q, PACK], BF16, name="w_grouped", offset=POOL_BYTES, align_bytes=64)
        weave(nc.vector.tensor_copy, w_turned, w_grouped[:])
        middle_codes = placed.tile([P, 2 * P], U32, name="middle_codes", offset=POOL_BYTES + ROW_BYTES, align_bytes=64)
        middle_scales = sb.tile([P, 2 * P], U8, name="middle_scales", align_bytes=64)
        quantise(middle_grouped[:], middle_codes[:], middle_scales[:])
        w_codes = sb.tile([P, Q], U32, name="w_codes", align_bytes=64)
        w_scales = sb.tile([P, Q], U8, name="w_scales", align_bytes=64)
        quantise(w_grouped[:], w_codes[:], w_scales[:])
        v3_grouped = sb.tile([P, P, PACK], BF16, name="v3_grouped", align_bytes=64)
        weave(nc.scalar.copy, turn(v3_listed, "v3_turned", "bank_a0"), v3_grouped[:])
        quantise(v3_grouped[:], outer_codes[:, P:], outer_scales[:, P:])

        out_tiles = out.rearrange("q (j e) -> q j e", e=P)
        for codes, scales, tiles, bank, copy, queue in (
            (middle_codes, middle_scales, slice(1, LAST), "bank_a0", nc.scalar.copy, nc.scalar),
            (outer_codes, outer_scales, slice(0, VALUE_TILES, LAST), "bank_a1", nc.vector.tensor_copy, nc.sync),
        ):
            acc = ps.tile([P, 2 * P], F32, name="acc_" + bank, tag=bank)
            product(acc[:], w_codes[:], w_scales[:], codes[:].bitcast(FP8X4), scales[:])
            result = sb.tile([P, 2, P], F32, name="result_" + bank)
            copy(result[:].rearrange("q j e -> q (j e)"), acc[:])
            queue.dma_start(out_tiles[:, tiles, :], result[:])
